import numpy as np
import ml_dtypes


def mxq(x, axis, fmt="e4m3"):
    dtype, down = {"e4m3": (ml_dtypes.float8_e4m3fn, 7), "e5m2": (ml_dtypes.float8_e5m2, 14)}[fmt]
    v = np.moveaxis(np.asarray(x, np.float32).astype(ml_dtypes.bfloat16).astype(np.float64), axis, -1)
    blocks = v.reshape(v.shape[:-1] + (-1, 32))
    amax = np.abs(blocks).max(-1, keepdims=True)
    byte = np.maximum(np.where(amax > 0, np.frexp(amax)[1] - 1 + 127, 0) - down, 1)
    scale = np.exp2(byte - 127.0)
    codes = (blocks / scale).astype(np.float32).astype(dtype).astype(np.float64)
    return np.moveaxis((codes * scale).reshape(v.shape), -1, axis)


WIDE = False


def mx_kscale(k):
    if not WIDE:
        return np.ones(k)
    levels = np.array([30, -30])
    if k % 512:
        return np.exp2(np.random.permutation(np.resize(levels, k // 32))).repeat(32)
    a = np.empty((k // 512, 16))
    for p in range(k // 512):
        a[p, :8] = np.random.permutation(np.resize(levels, 8))
        for g in range(8):
            far = levels[np.abs(levels - a[p, g]) >= 10]
            a[p, g + 8] = far[np.random.randint(len(far))]
    return np.exp2(a.ravel()).repeat(32)


def f64(x):
    return np.asarray(x).astype(np.float64)


def striped(idx):
    return np.tile(idx.reshape(-1, 16).T, (8, 1)).astype(np.uint16)


def unstriped(offs):
    return offs[:16].T.reshape(-1).astype(np.int64)


K, T, E, C, N = 128, 2048, 4, 512, 1536


def by_expert(wq, xq):
    return np.concatenate([wq[e].T @ xq[:, e * C:(e + 1) * C] for e in range(E)], axis=1)


def setup_inputs():
    n = np.random.standard_normal
    s = mx_kscale(N)[:, None]
    return {
        "dyT": (n((N, T)) * s).astype(np.float32),
        "w": (n((E, N, K)) / np.sqrt(N) / s[None]).astype(np.float32),
        "gate": np.tile(np.random.uniform(0.2, 1.0, E * C), (N, 1)).astype(np.float32),
        "offs": striped(np.random.permutation(T)[:E * C]),
    }


def reference(dyT, w, gate, offs):
    idx = unstriped(offs)
    gq = mxq(f64(gate) * f64(dyT)[:, idx], 0, "e5m2")
    dx = by_expert(mxq(f64(w), 1, "e4m3"), gq)
    out = np.zeros((K, T))
    out[:, idx] = dx
    return out

@@ -1,0 +1,186 @@
+from contextlib import ExitStack
+
+import concourse.mybir as mybir
+
+K, T, E, C, N = 128, 2048, 4, 512, 1536
+P = 128
+PACK = 4
+PASSES = N // (P * PACK)
+
+FLOPS = 2 * K * N * E * C
+BYTES = 4 * (N * T + E * N * K + T + K * T) + 2 * T
+
+F32 = mybir.dt.float32
+BF16 = mybir.dt.bfloat16
+U32 = mybir.dt.uint32
+U16 = mybir.dt.uint16
+U8 = mybir.dt.uint8
+E4M3 = mybir.dt.float8_e4m3fn_x4
+E5M2 = mybir.dt.float8_e5m2_x4
+MULT = mybir.AluOpType.mult
+
+
+def tile_moe_bdx_lin_none_kernel(tc, dyT, w, gate, offs, out):
+    nc = tc.nc
+    dy_rows = dyT.rearrange("(g p t) c -> g t p c", p=P, t=PACK)
+    w_rows = w.rearrange("e (g p t) k -> g p e t k", p=P, t=PACK)
+
+    with ExitStack() as ctx:
+        lists = ctx.enter_context(tc.tile_pool(name="lists", bufs=1))
+        keep = ctx.enter_context(tc.tile_pool(name="keep", bufs=1))
+        dys = ctx.enter_context(tc.tile_pool(name="dys", bufs=10))
+        raws = ctx.enter_context(tc.tile_pool(name="raws", bufs=2))
+        gath = ctx.enter_context(tc.tile_pool(name="gath", bufs=3))
+        grp = ctx.enter_context(tc.tile_pool(name="grp", bufs=4))
+        mxs = ctx.enter_context(tc.tile_pool(name="mxs", bufs=6))
+        psum = ctx.enter_context(tc.psum_pool(name="psum", bufs=1))
+
+        slots = lists.tile([P, E * C // 16], U16, name="slots")
+        gates = keep.tile([P, E * C], F32, name="gates")
+        window = keep.tile([P, T], F32, name="window")
+        w_codes = [keep.tile([P, E * K], U32, name=f"w_codes{g}", align_bytes=64) for g in range(PASSES)]
+        w_scales = [keep.tile([P, E * K], U8, name=f"w_scales{g}", align_bytes=64) for g in range(PASSES)]
+        results = [keep.tile([P, C], F32, name=f"result{e}") for e in range(E)]
+        banks = [psum.tile([P, C], F32, name=f"bank{e}") for e in range(E)]
+
+        dy = {}
+        w_raw = {}
+
+        def load_dy(g, t):
+            tile = dys.tile([P, T], F32, name="dy")
+            nc.sync.dma_start(out=tile[:], in_=dy_rows[g, t])
+            dy[g, t] = tile
+
+        def load_w(g):
+            tile = raws.tile([P, E, PACK, K], F32, name="w_raw")
+            for e in range(E):
+                nc.sync.dma_start(out=tile[:, e], in_=w_rows[g, :, e])
+            w_raw[g] = tile
+
+        def make_w(g):
+            grouped = grp.tile([P, E, K, PACK], BF16, name="grouped", align_bytes=64)
+            nc.scalar.copy(out=grouped[:], in_=w_raw[g][:].rearrange("p e t k -> p e k t"))
+            nc.vector.quantize_mx(
+                out=w_codes[g][:].bitcast(E4M3),
+                scales=w_scales[g][:],
+                in_=grouped[:].rearrange("p e k t -> p (e k t)"),
+            )
+
+        gathered = {}
+        grouped_g = {}
+        codes = {}
+
+        def gather(g, first, count):
+            tile = gath.tile([P, PACK, count], F32, name="gathered")
+            for t in range(PACK):
+                nc.vector.tensor_tensor(
+                    tile[:, t, :],
+                    dy[g, t][:].indirect(slots[:, first // 16 : (first + count) // 16]),
+                    gates[:, first : first + count],
+                    MULT,
+                )
+            return tile
+
+        def interleave(tile, grouped, src, dst, count):
+            nc.scalar.copy(
+                out=grouped[:, dst : dst + count, :],
+                in_=tile[:, :, src : src + count].rearrange("p t c -> p c t"),
+            )
+
+        def new_grouped():
+            return grp.tile([P, C, PACK], BF16, name="grouped", align_bytes=64)
+
+        def quantise(g, e, grouped, parts):
+            words = mxs.tile([P, C], U32, name="words", align_bytes=64)
+            scales = mxs.tile([P, C], U8, name="scales", align_bytes=64)
+            n = C // parts
+            for i in range(parts):
+                nc.vector.quantize_mx(
+                    out=words[:, i * n : (i + 1) * n].bitcast(E5M2),
+                    scales=scales[:, i * n : (i + 1) * n],
+                    in_=grouped[:, i * n : (i + 1) * n, :].rearrange("p c t -> p (c t)"),
+                )
+            nc.tensor.matmul_mx(
+                out=banks[e][:],
+                lhsT=w_codes[g][:, e * K : (e + 1) * K].bitcast(E4M3),
+                lhsT_scale=w_scales[g][:, e * K : (e + 1) * K],
+                rhs=words[:].bitcast(E5M2),
+                rhs_scale=scales[:],
+                start=(g == 0),
+                stop=(g == PASSES - 1),
+            )
+
+        def empty(e):
+            nc.scalar.copy(out=results[e][:], in_=banks[e][:])
+
+        def scatter(e):
+            nc.vector.tensor_copy(
+                window[:].indirect(slots[:, e * C // 16 : (e + 1) * C // 16]), results[e][:]
+            )
+
+        half = E * C // 2
+        nc.sync.dma_start(out=slots[:], in_=offs)
+        nc.sync.dma_start(out=gates[:, :half], in_=gate[0:P, :half])
+        load_dy(0, 0)
+        load_dy(0, 1)
+        nc.sync.dma_start(out=gates[:, half:], in_=gate[0:P, half:])
+        load_w(0)
+        load_dy(0, 2)
+        load_dy(0, 3)
+        load_dy(1, 0)
+        load_dy(1, 1)
+        load_w(1)
+        load_dy(1, 2)
+        load_dy(1, 3)
+        load_dy(2, 0)
+        load_dy(2, 1)
+        load_dy(2, 2)
+        load_dy(2, 3)
+        load_w(2)
+
+        make_w(0)
+        pending = []
+        for g in range(PASSES - 1):
+            tiles = [gath.tile([P, PACK, half], F32, name="gathered") for h in range(2)]
+            for t in range(PACK):
+                for h in range(2):
+                    nc.vector.tensor_tensor(
+                        tiles[h][:, t, :],
+                        dy[g, t][:].indirect(slots[:, h * half // 16 : (h + 1) * half // 16]),
+                        gates[:, h * half : (h + 1) * half],
+                        MULT,
+                    )
+            for item in pending:
+                quantise(*item)
+            pending = []
+            for e in range(E):
+                grouped = new_grouped()
+                interleave(tiles[e // 2], grouped, (e % 2) * C, 0, C)
+                pending.append((g, e, grouped, 1))
+            make_w(g + 1)
+        g = PASSES - 1
+        for e in range(E - 1):
+            tile = gather(g, e * C, C)
+            for item in pending:
+                quantise(*item)
+            grouped = new_grouped()
+            interleave(tile, grouped, 0, 0, C)
+            pending = [(g, e, grouped, 1)]
+            if e > 0:
+                empty(e - 1)
+        e = E - 1
+        grouped = new_grouped()
+        tile = gather(g, e * C, C // 2)
+        for item in pending:
+            quantise(*item)
+        interleave(tile, grouped, 0, 0, C // 2)
+        empty(e - 1)
+        tile = gather(g, e * C + C // 2, C // 2)
+        interleave(tile, grouped, 0, C // 2, C // 2)
+        scatter(0)
+        quantise(g, e, grouped, 2)
+        scatter(1)
+        scatter(2)
+        empty(e)
+        scatter(e)
+        nc.sync.dma_start(out=out, in_=window[:])

@@ -23,7 +23,7 @@ MULT = mybir.AluOpType.mult
 def tile_moe_bdx_lin_none_kernel(tc, dyT, w, gate, offs, out):
     nc = tc.nc
     dy_rows = dyT.rearrange("(g p t) c -> g t p c", p=P, t=PACK)
-    w_rows = w.rearrange("e (g p t) k -> g p e t k", p=P, t=PACK)
+    w_rows = w.rearrange("e (g p t) k -> g p e (t k)", p=P, t=PACK)
 
     with ExitStack() as ctx:
         lists = ctx.enter_context(tc.tile_pool(name="lists", bufs=1))
@@ -31,8 +31,8 @@ def tile_moe_bdx_lin_none_kernel(tc, dyT, w, gate, offs, out):
         dys = ctx.enter_context(tc.tile_pool(name="dys", bufs=10))
         raws = ctx.enter_context(tc.tile_pool(name="raws", bufs=2))
         gath = ctx.enter_context(tc.tile_pool(name="gath", bufs=3))
-        grp = ctx.enter_context(tc.tile_pool(name="grp", bufs=4))
-        mxs = ctx.enter_context(tc.tile_pool(name="mxs", bufs=6))
+        grp = ctx.enter_context(tc.tile_pool(name="grp", bufs=3))
+        mxs = ctx.enter_context(tc.tile_pool(name="mxs", bufs=3))
         psum = ctx.enter_context(tc.psum_pool(name="psum", bufs=1))
 
         slots = lists.tile([P, E * C // 16], U16, name="slots")
@@ -40,11 +40,13 @@ def tile_moe_bdx_lin_none_kernel(tc, dyT, w, gate, offs, out):
         window = keep.tile([P, T], F32, name="window")
         w_codes = [keep.tile([P, E * K], U32, name=f"w_codes{g}", align_bytes=64) for g in range(PASSES)]
         w_scales = [keep.tile([P, E * K], U8, name=f"w_scales{g}", align_bytes=64) for g in range(PASSES)]
-        results = [keep.tile([P, C], F32, name=f"result{e}") for e in range(E)]
         banks = [psum.tile([P, C], F32, name=f"bank{e}") for e in range(E)]
 
         dy = {}
         w_raw = {}
+
+        def load_gates(first, last):
+            nc.sync.dma_start(out=gates[:, first:last], in_=gate[0:P, first:last])
 
         def load_dy(g, t):
             tile = dys.tile([P, T], F32, name="dy")
@@ -53,12 +55,27 @@ def tile_moe_bdx_lin_none_kernel(tc, dyT, w, gate, offs, out):
 
         def load_w(g):
             tile = raws.tile([P, E, PACK, K], F32, name="w_raw")
-            for e in range(E):
-                nc.sync.dma_start(out=tile[:, e], in_=w_rows[g, :, e])
+            nc.sync.dma_start(out=tile[:].rearrange("p e t k -> p e (t k)"), in_=w_rows[g])
             w_raw[g] = tile
 
+        nc.sync.dma_start(out=slots[:], in_=offs)
+        load_gates(0, C)
+        load_dy(0, 0)
+        load_gates(C, 2 * C)
+        load_gates(2 * C, 4 * C)
+        load_dy(0, 1)
+        load_dy(0, 2)
+        load_w(0)
+        load_dy(0, 3)
+        for t in range(PACK):
+            load_dy(1, t)
+        load_w(1)
+        for t in range(PACK):
+            load_dy(2, t)
+        load_w(2)
+
         def make_w(g):
-            grouped = grp.tile([P, E, K, PACK], BF16, name="grouped", align_bytes=64)
+            grouped = grp.tile([P, E, K, PACK], BF16, name="w_grouped", align_bytes=64)
             nc.scalar.copy(out=grouped[:], in_=w_raw[g][:].rearrange("p e t k -> p e k t"))
             nc.vector.quantize_mx(
                 out=w_codes[g][:].bitcast(E4M3),
@@ -66,121 +83,101 @@ def tile_moe_bdx_lin_none_kernel(tc, dyT, w, gate, offs, out):
                 in_=grouped[:].rearrange("p e k t -> p (e k t)"),
             )
 
-        gathered = {}
-        grouped_g = {}
-        codes = {}
-
-        def gather(g, first, count):
-            tile = gath.tile([P, PACK, count], F32, name="gathered")
-            for t in range(PACK):
-                nc.vector.tensor_tensor(
-                    tile[:, t, :],
-                    dy[g, t][:].indirect(slots[:, first // 16 : (first + count) // 16]),
-                    gates[:, first : first + count],
-                    MULT,
-                )
-            return tile
-
-        def interleave(tile, grouped, src, dst, count):
-            nc.scalar.copy(
-                out=grouped[:, dst : dst + count, :],
-                in_=tile[:, :, src : src + count].rearrange("p t c -> p c t"),
+        def gather(tile, g, t, start, first, last):
+            nc.vector.tensor_tensor(
+                tile[:, t, first - start : last - start],
+                dy[g, t][:].indirect(slots[:, first // 16 : last // 16]),
+                gates[:, first:last],
+                MULT,
             )
 
-        def new_grouped():
-            return grp.tile([P, C, PACK], BF16, name="grouped", align_bytes=64)
-
-        def quantise(g, e, grouped, parts):
-            words = mxs.tile([P, C], U32, name="words", align_bytes=64)
-            scales = mxs.tile([P, C], U8, name="scales", align_bytes=64)
-            n = C // parts
-            for i in range(parts):
-                nc.vector.quantize_mx(
-                    out=words[:, i * n : (i + 1) * n].bitcast(E5M2),
-                    scales=scales[:, i * n : (i + 1) * n],
-                    in_=grouped[:, i * n : (i + 1) * n, :].rearrange("p c t -> p (c t)"),
+        def interleave(tile, n):
+            grouped = grp.tile([P, n, PACK], BF16, name="grouped", align_bytes=64)
+            for i in range(0, n, C):
+                nc.scalar.copy(
+                    out=grouped[:, i : i + C, :],
+                    in_=tile[:, :, i : i + C].rearrange("p t c -> p c t"),
                 )
-            nc.tensor.matmul_mx(
-                out=banks[e][:],
-                lhsT=w_codes[g][:, e * K : (e + 1) * K].bitcast(E4M3),
-                lhsT_scale=w_scales[g][:, e * K : (e + 1) * K],
-                rhs=words[:].bitcast(E5M2),
-                rhs_scale=scales[:],
-                start=(g == 0),
-                stop=(g == PASSES - 1),
+            return grouped
+
+        def multiply(g, first, n, grouped):
+            words = mxs.tile([P, n], U32, name="words", align_bytes=64)
+            scales = mxs.tile([P, n], U8, name="scales", align_bytes=64)
+            nc.vector.quantize_mx(
+                out=words[:].bitcast(E5M2),
+                scales=scales[:],
+                in_=grouped[:].rearrange("p c t -> p (c t)"),
             )
+            for i in range(0, n, C):
+                e = (first + i) // C
+                nc.tensor.matmul_mx(
+                    out=banks[e][:],
+                    lhsT=w_codes[g][:, e * K : (e + 1) * K].bitcast(E4M3),
+                    lhsT_scale=w_scales[g][:, e * K : (e + 1) * K],
+                    rhs=words[:, i : i + C].bitcast(E5M2),
+                    rhs_scale=scales[:, i : i + C],
+                    start=(g == 0),
+                    stop=(g == PASSES - 1),
+                )
 
-        def empty(e):
-            nc.scalar.copy(out=results[e][:], in_=banks[e][:])
+        results = {}
 
-        def scatter(e):
+        def empty(first, n):
+            result = keep.tile([P, n], F32, name=f"result{first}")
+            for i in range(0, n, C):
+                nc.scalar.copy(out=result[:, i : i + C], in_=banks[(first + i) // C][:])
+            results[first] = result
+
+        def scatter(first, n):
             nc.vector.tensor_copy(
-                window[:].indirect(slots[:, e * C // 16 : (e + 1) * C // 16]), results[e][:]
+                window[:].indirect(slots[:, first // 16 : (first + n) // 16]), results[first][:]
             )
-
-        half = E * C // 2
-        nc.sync.dma_start(out=slots[:], in_=offs)
-        nc.sync.dma_start(out=gates[:, :half], in_=gate[0:P, :half])
-        load_dy(0, 0)
-        load_dy(0, 1)
-        nc.sync.dma_start(out=gates[:, half:], in_=gate[0:P, half:])
-        load_w(0)
-        load_dy(0, 2)
-        load_dy(0, 3)
-        load_dy(1, 0)
-        load_dy(1, 1)
-        load_w(1)
-        load_dy(1, 2)
-        load_dy(1, 3)
-        load_dy(2, 0)
-        load_dy(2, 1)
-        load_dy(2, 2)
-        load_dy(2, 3)
-        load_w(2)
 
         make_w(0)
-        pending = []
-        for g in range(PASSES - 1):
-            tiles = [gath.tile([P, PACK, half], F32, name="gathered") for h in range(2)]
-            for t in range(PACK):
-                for h in range(2):
-                    nc.vector.tensor_tensor(
-                        tiles[h][:, t, :],
-                        dy[g, t][:].indirect(slots[:, h * half // 16 : (h + 1) * half // 16]),
-                        gates[:, h * half : (h + 1) * half],
-                        MULT,
-                    )
-            for item in pending:
-                quantise(*item)
-            pending = []
-            for e in range(E):
-                grouped = new_grouped()
-                interleave(tiles[e // 2], grouped, (e % 2) * C, 0, C)
-                pending.append((g, e, grouped, 1))
-            make_w(g + 1)
-        g = PASSES - 1
-        for e in range(E - 1):
-            tile = gather(g, e * C, C)
-            for item in pending:
-                quantise(*item)
-            grouped = new_grouped()
-            interleave(tile, grouped, 0, 0, C)
-            pending = [(g, e, grouped, 1)]
-            if e > 0:
-                empty(e - 1)
-        e = E - 1
-        grouped = new_grouped()
-        tile = gather(g, e * C, C // 2)
-        for item in pending:
-            quantise(*item)
-        interleave(tile, grouped, 0, 0, C // 2)
-        empty(e - 1)
-        tile = gather(g, e * C + C // 2, C // 2)
-        interleave(tile, grouped, 0, C // 2, C // 2)
-        scatter(0)
-        quantise(g, e, grouped, 2)
-        scatter(1)
-        scatter(2)
-        empty(e)
-        scatter(e)
+        half = 2 * C
+        low = gath.tile([P, PACK, half], F32, name="gathered")
+        high = gath.tile([P, PACK, half], F32, name="gathered")
+        gather(low, 0, 0, 0, 0, C)
+        gather(low, 0, 0, 0, C, half)
+        gather(high, 0, 0, half, half, 2 * half)
+        for t in range(1, PACK):
+            gather(low, 0, t, 0, 0, half)
+            gather(high, 0, t, half, half, 2 * half)
+        g_low = interleave(low, half)
+        make_w(1)
+        g_high = interleave(high, half)
+        low = gath.tile([P, PACK, half], F32, name="gathered")
+        for t in range(PACK):
+            gather(low, 1, t, 0, 0, half)
+        multiply(0, 0, half, g_low)
+        g_low = interleave(low, half)
+        high = gath.tile([P, PACK, half], F32, name="gathered")
+        for t in range(PACK):
+            gather(high, 1, t, half, half, 2 * half)
+        multiply(0, half, half, g_high)
+        make_w(2)
+        g_high = interleave(high, half)
+        low = gath.tile([P, PACK, half], F32, name="gathered")
+        for t in range(PACK):
+            gather(low, 2, t, 0, 0, half)
+        multiply(1, 0, half, g_low)
+        g_low = interleave(low, half)
+        third = gath.tile([P, PACK, C], F32, name="gathered")
+        for t in range(PACK):
+            gather(third, 2, t, half, half, half + C)
+        multiply(1, half, half, g_high)
+        multiply(2, 0, half, g_low)
+        g_third = interleave(third, C)
+        empty(0, half)
+        fourth = gath.tile([P, PACK, C], F32, name="gathered")
+        for t in range(PACK):
+            gather(fourth, 2, t, half + C, half + C, 2 * half)
+        multiply(2, half, C, g_third)
+        g_fourth = interleave(fourth, C)
+        scatter(0, half)
+        empty(half, C)
+        multiply(2, half + C, C, g_fourth)
+        scatter(half, C)
+        empty(half + C, C)
+        scatter(half + C, C)
         nc.sync.dma_start(out=out, in_=window[:])

@@ -3,12 +3,18 @@ from contextlib import ExitStack
 import concourse.mybir as mybir
 
 K, T, E, C, N = 128, 2048, 4, 512, 1536
+SLOTS = E * C
 P = 128
-PACK = 4
-PASSES = N // (P * PACK)
+PLANES = 4
+PASSES = N // (P * PLANES)
+OFFSETS = 16
+HALF = SLOTS // 2
+RUN = 4
 
-FLOPS = 2 * K * N * E * C
-BYTES = 4 * (N * T + E * N * K + T + K * T) + 2 * T
+FIRST_CUTS = (0, 128, C, HALF, SLOTS)
+
+FLOPS = 2 * K * N * SLOTS
+BYTES = 4 * (N * T + E * N * K + SLOTS + K * T) + 2 * SLOTS
 
 F32 = mybir.dt.float32
 BF16 = mybir.dt.bfloat16
@@ -17,29 +23,31 @@ U16 = mybir.dt.uint16
 U8 = mybir.dt.uint8
 E4M3 = mybir.dt.float8_e4m3fn_x4
 E5M2 = mybir.dt.float8_e5m2_x4
-MULT = mybir.AluOpType.mult
 
 
 def tile_moe_bdx_lin_none_kernel(tc, dyT, w, gate, offs, out):
     nc = tc.nc
-    dy_rows = dyT.rearrange("(g p t) c -> g t p c", p=P, t=PACK)
-    w_rows = w.rearrange("e (g p t) k -> g p e (t k)", p=P, t=PACK)
+    dy_rows = dyT.rearrange("(g p t) c -> g t p c", p=P, t=PLANES)
+    w_rows = w.rearrange("e (g p t) k -> g p e (t k)", p=P, t=PLANES)
 
     with ExitStack() as ctx:
         lists = ctx.enter_context(tc.tile_pool(name="lists", bufs=1))
         keep = ctx.enter_context(tc.tile_pool(name="keep", bufs=1))
-        dys = ctx.enter_context(tc.tile_pool(name="dys", bufs=10))
-        raws = ctx.enter_context(tc.tile_pool(name="raws", bufs=2))
-        gath = ctx.enter_context(tc.tile_pool(name="gath", bufs=3))
-        grp = ctx.enter_context(tc.tile_pool(name="grp", bufs=3))
-        mxs = ctx.enter_context(tc.tile_pool(name="mxs", bufs=3))
+        dy_pool = ctx.enter_context(tc.tile_pool(name="dy_pool", bufs=8))
+        w_raw_pool = ctx.enter_context(tc.tile_pool(name="w_raw_pool", bufs=2))
+        w_side_pool = ctx.enter_context(tc.tile_pool(name="w_side_pool", bufs=2))
+        half_pool = ctx.enter_context(tc.tile_pool(name="half_pool", bufs=3))
+        expert_pool = ctx.enter_context(tc.tile_pool(name="expert_pool", bufs=3))
+        side_pool = ctx.enter_context(tc.tile_pool(name="side_pool", bufs=3))
+        code_pool = ctx.enter_context(tc.tile_pool(name="code_pool", bufs=3))
         psum = ctx.enter_context(tc.psum_pool(name="psum", bufs=1))
 
-        slots = lists.tile([P, E * C // 16], U16, name="slots")
-        gates = keep.tile([P, E * C], F32, name="gates")
-        window = keep.tile([P, T], F32, name="window")
+        offsets = lists.tile([P, SLOTS // OFFSETS], U16, name="offsets")
+        gates = keep.tile([P, SLOTS], F32, name="gates")
+        tokens = keep.tile([P, T], F32, name="tokens")
         w_codes = [keep.tile([P, E * K], U32, name=f"w_codes{g}", align_bytes=64) for g in range(PASSES)]
         w_scales = [keep.tile([P, E * K], U8, name=f"w_scales{g}", align_bytes=64) for g in range(PASSES)]
+        results = [keep.tile([P, C], F32, name=f"result{e}") for e in range(E)]
         banks = [psum.tile([P, C], F32, name=f"bank{e}") for e in range(E)]
 
         dy = {}
@@ -49,135 +57,128 @@ def tile_moe_bdx_lin_none_kernel(tc, dyT, w, gate, offs, out):
             nc.sync.dma_start(out=gates[:, first:last], in_=gate[0:P, first:last])
 
         def load_dy(g, t):
-            tile = dys.tile([P, T], F32, name="dy")
-            nc.sync.dma_start(out=tile[:], in_=dy_rows[g, t])
-            dy[g, t] = tile
+            dy[g, t] = dy_pool.tile([P, T], F32, name="dy_block")
+            nc.sync.dma_start(out=dy[g, t][:], in_=dy_rows[g, t])
 
         def load_w(g):
-            tile = raws.tile([P, E, PACK, K], F32, name="w_raw")
-            nc.sync.dma_start(out=tile[:].rearrange("p e t k -> p e (t k)"), in_=w_rows[g])
-            w_raw[g] = tile
+            w_raw[g] = w_raw_pool.tile([P, E, PLANES, K], F32, name="w_block")
+            nc.sync.dma_start(out=w_raw[g][:].rearrange("p e t k -> p e (t k)"), in_=w_rows[g])
 
-        nc.sync.dma_start(out=slots[:], in_=offs)
-        load_gates(0, C)
+        nc.sync.dma_start(out=offsets[:], in_=offs)
+        load_gates(FIRST_CUTS[0], FIRST_CUTS[1])
         load_dy(0, 0)
-        load_gates(C, 2 * C)
-        load_gates(2 * C, 4 * C)
+        for first, last in zip(FIRST_CUTS[1:], FIRST_CUTS[2:]):
+            load_gates(first, last)
         load_dy(0, 1)
         load_dy(0, 2)
         load_w(0)
         load_dy(0, 3)
-        for t in range(PACK):
-            load_dy(1, t)
-        load_w(1)
-        for t in range(PACK):
-            load_dy(2, t)
-        load_w(2)
+        for g in range(1, PASSES):
+            for t in range(PLANES):
+                load_dy(g, t)
+            load_w(g)
 
-        def make_w(g):
-            grouped = grp.tile([P, E, K, PACK], BF16, name="w_grouped", align_bytes=64)
-            nc.scalar.copy(out=grouped[:], in_=w_raw[g][:].rearrange("p e t k -> p e k t"))
+        def side_by_side(grouped, planes):
+            nc.scalar.copy(
+                out=grouped.rearrange("p (c i) t -> p c t i", i=RUN),
+                in_=planes.rearrange("p t (c i) -> p c t i", i=RUN),
+            )
+
+        def quantise_w(g):
+            grouped = w_side_pool.tile([P, E, K, PLANES], BF16, name="w_grouped", align_bytes=64)
+            for e in range(E):
+                side_by_side(grouped[:, e], w_raw[g][:, e])
             nc.vector.quantize_mx(
                 out=w_codes[g][:].bitcast(E4M3),
                 scales=w_scales[g][:],
                 in_=grouped[:].rearrange("p e k t -> p (e k t)"),
             )
 
-        def gather(tile, g, t, start, first, last):
+        gathered = {}
+        interleaved = {}
+
+        def open_unit(unit):
+            count = unit[2]
+            pool = half_pool if count == HALF else expert_pool
+            gathered[unit] = pool.tile([P, PLANES, count], F32, name="gathered_planes")
+
+        def gather(unit, t, first, last):
+            g, start, count = unit
             nc.vector.tensor_tensor(
-                tile[:, t, first - start : last - start],
-                dy[g, t][:].indirect(slots[:, first // 16 : last // 16]),
+                gathered[unit][:, t, first - start : last - start],
+                dy[g, t][:].indirect(offsets[:, first // OFFSETS : last // OFFSETS]),
                 gates[:, first:last],
-                MULT,
+                mybir.AluOpType.mult,
             )
 
-        def interleave(tile, n):
-            grouped = grp.tile([P, n, PACK], BF16, name="grouped", align_bytes=64)
-            for i in range(0, n, C):
-                nc.scalar.copy(
-                    out=grouped[:, i : i + C, :],
-                    in_=tile[:, :, i : i + C].rearrange("p t c -> p c t"),
-                )
-            return grouped
+        def interleave(unit):
+            count = unit[2]
+            interleaved[unit] = side_pool.tile([P, count, PLANES], BF16, name="grouped", align_bytes=64)
+            for c in range(0, count, C):
+                side_by_side(interleaved[unit][:, c : c + C], gathered[unit][:, :, c : c + C])
 
-        def multiply(g, first, n, grouped):
-            words = mxs.tile([P, n], U32, name="words", align_bytes=64)
-            scales = mxs.tile([P, n], U8, name="scales", align_bytes=64)
+        def multiply(unit):
+            g, start, count = unit
+            codes = code_pool.tile([P, count], U32, name="codes", align_bytes=64)
+            scales = code_pool.tile([P, count], U8, name="scales", align_bytes=64)
             nc.vector.quantize_mx(
-                out=words[:].bitcast(E5M2),
+                out=codes[:].bitcast(E5M2),
                 scales=scales[:],
-                in_=grouped[:].rearrange("p c t -> p (c t)"),
+                in_=interleaved[unit][:].rearrange("p c t -> p (c t)"),
             )
-            for i in range(0, n, C):
-                e = (first + i) // C
+            for c in range(0, count, C):
+                e = (start + c) // C
                 nc.tensor.matmul_mx(
                     out=banks[e][:],
                     lhsT=w_codes[g][:, e * K : (e + 1) * K].bitcast(E4M3),
                     lhsT_scale=w_scales[g][:, e * K : (e + 1) * K],
-                    rhs=words[:, i : i + C].bitcast(E5M2),
-                    rhs_scale=scales[:, i : i + C],
+                    rhs=codes[:, c : c + C].bitcast(E5M2),
+                    rhs_scale=scales[:, c : c + C],
                     start=(g == 0),
                     stop=(g == PASSES - 1),
                 )
 
-        results = {}
+        def finish(unit):
+            e = unit[1] // C
+            nc.scalar.copy(out=results[e][:], in_=banks[e][:])
 
-        def empty(first, n):
-            result = keep.tile([P, n], F32, name=f"result{first}")
-            for i in range(0, n, C):
-                nc.scalar.copy(out=result[:, i : i + C], in_=banks[(first + i) // C][:])
-            results[first] = result
-
-        def scatter(first, n):
+        def scatter(e):
             nc.vector.tensor_copy(
-                window[:].indirect(slots[:, first // 16 : (first + n) // 16]), results[first][:]
+                tokens[:].indirect(offsets[:, e * C // OFFSETS : (e + 1) * C // OFFSETS]), results[e][:]
             )
 
-        make_w(0)
-        half = 2 * C
-        low = gath.tile([P, PACK, half], F32, name="gathered")
-        high = gath.tile([P, PACK, half], F32, name="gathered")
-        gather(low, 0, 0, 0, 0, C)
-        gather(low, 0, 0, 0, C, half)
-        gather(high, 0, 0, half, half, 2 * half)
-        for t in range(1, PACK):
-            gather(low, 0, t, 0, 0, half)
-            gather(high, 0, t, half, half, 2 * half)
-        g_low = interleave(low, half)
-        make_w(1)
-        g_high = interleave(high, half)
-        low = gath.tile([P, PACK, half], F32, name="gathered")
-        for t in range(PACK):
-            gather(low, 1, t, 0, 0, half)
-        multiply(0, 0, half, g_low)
-        g_low = interleave(low, half)
-        high = gath.tile([P, PACK, half], F32, name="gathered")
-        for t in range(PACK):
-            gather(high, 1, t, half, half, 2 * half)
-        multiply(0, half, half, g_high)
-        make_w(2)
-        g_high = interleave(high, half)
-        low = gath.tile([P, PACK, half], F32, name="gathered")
-        for t in range(PACK):
-            gather(low, 2, t, 0, 0, half)
-        multiply(1, 0, half, g_low)
-        g_low = interleave(low, half)
-        third = gath.tile([P, PACK, C], F32, name="gathered")
-        for t in range(PACK):
-            gather(third, 2, t, half, half, half + C)
-        multiply(1, half, half, g_high)
-        multiply(2, 0, half, g_low)
-        g_third = interleave(third, C)
-        empty(0, half)
-        fourth = gath.tile([P, PACK, C], F32, name="gathered")
-        for t in range(PACK):
-            gather(fourth, 2, t, half + C, half + C, 2 * half)
-        multiply(2, half, C, g_third)
-        g_fourth = interleave(fourth, C)
-        scatter(0, half)
-        empty(half, C)
-        multiply(2, half + C, C, g_fourth)
-        scatter(half, C)
-        empty(half + C, C)
-        scatter(half + C, C)
-        nc.sync.dma_start(out=out, in_=window[:])
+        first_units = [(0, start, HALF) for start in range(0, SLOTS, HALF)]
+        for unit in first_units:
+            open_unit(unit)
+        quantise_w(0)
+        for t in range(PLANES):
+            cuts = FIRST_CUTS if t == 0 else (0, HALF, SLOTS)
+            for first, last in zip(cuts, cuts[1:]):
+                gather(first_units[first // HALF], t, first, last)
+        for unit in first_units:
+            interleave(unit)
+
+        units = list(first_units)
+        for g in range(1, PASSES):
+            size = C if g == PASSES - 1 else HALF
+            for start in range(0, SLOTS, size):
+                unit = (g, start, size)
+                units.append(unit)
+                open_unit(unit)
+                for t in range(PLANES):
+                    gather(unit, t, start, start + size)
+                earlier = units[-3]
+                multiply(earlier)
+                interleave(unit)
+                if start == 0:
+                    quantise_w(g)
+                if earlier[0] == PASSES - 1:
+                    finish(earlier)
+
+        last_units = units[-2:]
+        for e in range(E):
+            scatter(e)
+            if e < len(last_units):
+                multiply(last_units[e])
+                finish(last_units[e])
+        nc.sync.dma_start(out=out, in_=tokens[:])

from contextlib import ExitStack

import concourse.mybir as mybir

K, T, E, C, N = 128, 2048, 4, 512, 1536
SLOTS = E * C
P = 128
PLANES = 4
PASSES = N // (P * PLANES)
OFFSETS = 16
HALF = SLOTS // 2
RUN = 4

FIRST_CUTS = (0, 128, C, HALF, SLOTS)

FLOPS = 2 * K * N * SLOTS
BYTES = 4 * (N * T + E * N * K + SLOTS + K * T) + 2 * SLOTS

F32 = mybir.dt.float32
BF16 = mybir.dt.bfloat16
U32 = mybir.dt.uint32
U16 = mybir.dt.uint16
U8 = mybir.dt.uint8
E4M3 = mybir.dt.float8_e4m3fn_x4
E5M2 = mybir.dt.float8_e5m2_x4


def tile_moe_bdx_lin_none_kernel(tc, dyT, w, gate, offs, out):
    nc = tc.nc
    dy_rows = dyT.rearrange("(g p t) c -> g t p c", p=P, t=PLANES)
    w_rows = w.rearrange("e (g p t) k -> g p e (t k)", p=P, t=PLANES)

    with ExitStack() as ctx:
        lists = ctx.enter_context(tc.tile_pool(name="lists", bufs=1))
        keep = ctx.enter_context(tc.tile_pool(name="keep", bufs=1))
        dy_pool = ctx.enter_context(tc.tile_pool(name="dy_pool", bufs=8))
        w_raw_pool = ctx.enter_context(tc.tile_pool(name="w_raw_pool", bufs=2))
        w_side_pool = ctx.enter_context(tc.tile_pool(name="w_side_pool", bufs=2))
        half_pool = ctx.enter_context(tc.tile_pool(name="half_pool", bufs=3))
        expert_pool = ctx.enter_context(tc.tile_pool(name="expert_pool", bufs=3))
        side_pool = ctx.enter_context(tc.tile_pool(name="side_pool", bufs=3))
        code_pool = ctx.enter_context(tc.tile_pool(name="code_pool", bufs=3))
        psum = ctx.enter_context(tc.psum_pool(name="psum", bufs=1))

        offsets = lists.tile([P, SLOTS // OFFSETS], U16, name="offsets")
        gates = keep.tile([P, SLOTS], F32, name="gates")
        tokens = keep.tile([P, T], F32, name="tokens")
        w_codes = [keep.tile([P, E * K], U32, name=f"w_codes{g}", align_bytes=64) for g in range(PASSES)]
        w_scales = [keep.tile([P, E * K], U8, name=f"w_scales{g}", align_bytes=64) for g in range(PASSES)]
        results = [keep.tile([P, C], F32, name=f"result{e}") for e in range(E)]
        banks = [psum.tile([P, C], F32, name=f"bank{e}") for e in range(E)]

        dy = {}
        w_raw = {}

        def load_gates(first, last):
            nc.sync.dma_start(out=gates[:, first:last], in_=gate[0:P, first:last])

        def load_dy(g, t):
            dy[g, t] = dy_pool.tile([P, T], F32, name="dy_block")
            nc.sync.dma_start(out=dy[g, t][:], in_=dy_rows[g, t])

        def load_w(g):
            w_raw[g] = w_raw_pool.tile([P, E, PLANES, K], F32, name="w_block")
            nc.sync.dma_start(out=w_raw[g][:].rearrange("p e t k -> p e (t k)"), in_=w_rows[g])

        nc.sync.dma_start(out=offsets[:], in_=offs)
        load_gates(FIRST_CUTS[0], FIRST_CUTS[1])
        load_dy(0, 0)
        for first, last in zip(FIRST_CUTS[1:], FIRST_CUTS[2:]):
            load_gates(first, last)
        load_dy(0, 1)
        load_dy(0, 2)
        load_w(0)
        load_dy(0, 3)
        for g in range(1, PASSES):
            for t in range(PLANES):
                load_dy(g, t)
            load_w(g)

        def side_by_side(grouped, planes):
            nc.scalar.copy(
                out=grouped.rearrange("p (c i) t -> p c t i", i=RUN),
                in_=planes.rearrange("p t (c i) -> p c t i", i=RUN),
            )

        def quantise_w(g):
            grouped = w_side_pool.tile([P, E, K, PLANES], BF16, name="w_grouped", align_bytes=64)
            for e in range(E):
                side_by_side(grouped[:, e], w_raw[g][:, e])
            nc.vector.quantize_mx(
                out=w_codes[g][:].bitcast(E4M3),
                scales=w_scales[g][:],
                in_=grouped[:].rearrange("p e k t -> p (e k t)"),
            )

        gathered = {}
        interleaved = {}

        def open_unit(unit):
            count = unit[2]
            pool = half_pool if count == HALF else expert_pool
            gathered[unit] = pool.tile([P, PLANES, count], F32, name="gathered_planes")

        def gather(unit, t, first, last):
            g, start, count = unit
            nc.vector.tensor_tensor(
                gathered[unit][:, t, first - start : last - start],
                dy[g, t][:].indirect(offsets[:, first // OFFSETS : last // OFFSETS]),
                gates[:, first:last],
                mybir.AluOpType.mult,
            )

        def interleave(unit):
            count = unit[2]
            interleaved[unit] = side_pool.tile([P, count, PLANES], BF16, name="grouped", align_bytes=64)
            for c in range(0, count, C):
                side_by_side(interleaved[unit][:, c : c + C], gathered[unit][:, :, c : c + C])

        def multiply(unit):
            g, start, count = unit
            codes = code_pool.tile([P, count], U32, name="codes", align_bytes=64)
            scales = code_pool.tile([P, count], U8, name="scales", align_bytes=64)
            nc.vector.quantize_mx(
                out=codes[:].bitcast(E5M2),
                scales=scales[:],
                in_=interleaved[unit][:].rearrange("p c t -> p (c t)"),
            )
            for c in range(0, count, C):
                e = (start + c) // C
                nc.tensor.matmul_mx(
                    out=banks[e][:],
                    lhsT=w_codes[g][:, e * K : (e + 1) * K].bitcast(E4M3),
                    lhsT_scale=w_scales[g][:, e * K : (e + 1) * K],
                    rhs=codes[:, c : c + C].bitcast(E5M2),
                    rhs_scale=scales[:, c : c + C],
                    start=(g == 0),
                    stop=(g == PASSES - 1),
                )

        def finish(unit):
            e = unit[1] // C
            nc.scalar.copy(out=results[e][:], in_=banks[e][:])

        def scatter(e):
            nc.vector.tensor_copy(
                tokens[:].indirect(offsets[:, e * C // OFFSETS : (e + 1) * C // OFFSETS]), results[e][:]
            )

        first_units = [(0, start, HALF) for start in range(0, SLOTS, HALF)]
        for unit in first_units:
            open_unit(unit)
        quantise_w(0)
        for t in range(PLANES):
            cuts = FIRST_CUTS if t == 0 else (0, HALF, SLOTS)
            for first, last in zip(cuts, cuts[1:]):
                gather(first_units[first // HALF], t, first, last)
        for unit in first_units:
            interleave(unit)

        units = list(first_units)
        for g in range(1, PASSES):
            size = C if g == PASSES - 1 else HALF
            for start in range(0, SLOTS, size):
                unit = (g, start, size)
                units.append(unit)
                open_unit(unit)
                for t in range(PLANES):
                    gather(unit, t, start, start + size)
                earlier = units[-3]
                multiply(earlier)
                interleave(unit)
                if start == 0:
                    quantise_w(g)
                if earlier[0] == PASSES - 1:
                    finish(earlier)

        last_units = units[-2:]
        for e in range(E):
            scatter(e)
            if e < len(last_units):
                multiply(last_units[e])
                finish(last_units[e])
        nc.sync.dma_start(out=out, in_=tokens[:])
